import numpy as np
import ml_dtypes


def mxq(x, axis, fmt="e4m3"):
    dtype, down = {"e4m3": (ml_dtypes.float8_e4m3fn, 7), "e5m2": (ml_dtypes.float8_e5m2, 14)}[fmt]
    v = np.moveaxis(np.asarray(x, np.float32).astype(ml_dtypes.bfloat16).astype(np.float64), axis, -1)
    blocks = v.reshape(v.shape[:-1] + (-1, 32))
    amax = np.abs(blocks).max(-1, keepdims=True)
    byte = np.maximum(np.where(amax > 0, np.frexp(amax)[1] - 1 + 127, 0) - down, 1)
    scale = np.exp2(byte - 127.0)
    codes = (blocks / scale).astype(np.float32).astype(dtype).astype(np.float64)
    return np.moveaxis((codes * scale).reshape(v.shape), -1, axis)


WIDE = False


def mx_kscale(k):
    if not WIDE:
        return np.ones(k)
    levels = np.array([10, -10, 5, -5, 0])
    if k % 512:
        return np.exp2(np.random.permutation(np.resize(levels, k // 32))).repeat(32)
    a = np.empty((k // 512, 16))
    for p in range(k // 512):
        a[p, :8] = np.random.permutation(np.resize(levels, 8))
        for g in range(8):
            far = levels[np.abs(levels - a[p, g]) >= 10]
            a[p, g + 8] = far[np.random.randint(len(far))]
    return np.exp2(a.ravel()).repeat(32)


def f64(x):
    return np.asarray(x).astype(np.float64)


def striped(idx):
    return np.tile(np.asarray(idx).reshape(-1, 16).T, (8, 1)).astype(np.uint16)


def unstriped(offs):
    return offs[:16].T.reshape(-1).astype(np.int64)


E2M1 = np.array([0.0, 0.5, 1.0, 1.5, 2.0, 3.0, 4.0, 6.0, -0.0, -0.5, -1.0, -1.5, -2.0, -3.0, -4.0, -6.0])


def pack_weight(w, fmt):
    k, n = w.shape
    w = f64(np.asarray(w, np.float32).astype(ml_dtypes.bfloat16)).reshape(k // 32, 32, n)
    amax = np.abs(w).max(1)
    if fmt == "e4m3":
        byte = np.frexp(amax)[1] - 1 + 127 - 7
    else:
        mant, ex = np.frexp(amax / 6.0)
        byte = np.where(mant > 0.5, ex, ex - 1) + 127
    byte = np.clip(np.where(amax > 0, byte, 1), 1, 254)
    scaled = (w * np.exp2(127.0 - byte)[:, None, :]).reshape(k, n).astype(np.float32)
    by_word = np.ascontiguousarray(scaled.reshape(k // 512, 128, 4, n).transpose(0, 1, 3, 2))
    if fmt == "e4m3":
        words = by_word.astype(ml_dtypes.float8_e4m3fn).view(np.uint8)
    else:
        c = by_word.astype(ml_dtypes.float4_e2m1fn).view(np.uint8) & 0xF
        words = (c[..., 0::2] | (c[..., 1::2] << 4)).reshape(k // 512, 128, 2 * n)
    return np.ascontiguousarray(words), np.ascontiguousarray(byte.astype(np.uint8).reshape(k // 512, 16, n))


def unpack_weight(words, scales, fmt):
    g, _, n = scales.shape
    words = np.ascontiguousarray(words).reshape(g, 128, n, -1)
    if fmt == "e4m3":
        vals = words.view(ml_dtypes.float8_e4m3fn).astype(np.float64)
    else:
        nib = np.empty((g, 128, n, 4), np.uint8)
        nib[..., 0::2] = words & 0xF
        nib[..., 1::2] = words >> 4
        vals = E2M1[nib]
    vals = vals * np.repeat(np.exp2(scales.astype(np.float64) - 127.0), 8, axis=1)[..., None]
    return vals.transpose(0, 1, 3, 2).reshape(g * 512, n)


def bf(x):
    return np.asarray(x, np.float32).astype(ml_dtypes.bfloat16)


def planes(Y):
    r, m = Y.shape
    b = f64(bf(Y)).reshape(r // 32, 32, m)
    amax = np.abs(b).max(1)
    byte = np.clip(np.where(amax > 0, np.frexp(amax)[1] - 1 + 127 - 7, 1), 1, 254)
    codes = (b * np.exp2(127.0 - byte)[:, None, :]).reshape(r, m).astype(np.float32).astype(ml_dtypes.float8_e4m3fn).view(np.uint8)
    words = codes.reshape(r // 512, 128, 4, m).transpose(0, 1, 3, 2)
    return np.ascontiguousarray(words), np.ascontiguousarray(byte.astype(np.uint8).reshape(r // 512, 16, m))


D, T, I, J, U, M, N = 512, 2048, 512, 512, 1024, 512, 64


def setup_inputs():
    n = np.random.standard_normal
    idx = np.random.permutation(T)[:I]
    idx2 = np.random.permutation(U)[:J]
    idx3 = np.random.permutation(U)[:J]
    idx4 = np.random.permutation(M)[:N]
    fd = mx_kscale(D)
    keysp = pack_weight(n((D, T)) / fd[:, None], "e2m1")
    return {
        "keys_words": keysp[0],
        "keys_scales": keysp[1],
        "notes": (n((D, U)) * 1.0 / np.sqrt(D) * fd[:, None]).astype(np.float32),
        "old": (1.0 * n((I, M))).astype(np.float32),
        "offs": striped(idx),
        "offs2": striped(idx2),
        "offs3": striped(idx3),
        "offs4": striped(idx4),
    }


def reference(keys_words, keys_scales, notes, old, offs, offs2, offs3, offs4):
    idx = unstriped(offs)
    idx2 = unstriped(offs2)
    idx3 = unstriped(offs3)
    idx4 = unstriped(offs4)
    keysu = unpack_weight(keys_words, keys_scales, "e2m1")
    keysidxg = keysu[:, idx]
    notesq = mxq(f64(notes), 0, "e4m3")
    g1 = keysidxg.T @ notesq
    g0 = g1[:, idx2] * g1[:, idx3]
    rb0 = g0.reshape(I, N, J // N).max(axis=2)
    gf = np.zeros((I, M))
    gf[:, idx4] = rb0
    y = f64(old) + gf
    words, scales = planes(y)
    return y, words, scales

@@ -1,0 +1,214 @@
+from contextlib import ExitStack
+
+import concourse.mybir as mybir
+
+D, T, I, J, U, M, N = 512, 2048, 512, 512, 1024, 512, 64
+FLOPS = 2 * D * I * U
+
+F32 = mybir.dt.float32
+BF16 = mybir.dt.bfloat16
+I32 = mybir.dt.int32
+U32 = mybir.dt.uint32
+U16 = mybir.dt.uint16
+U8 = mybir.dt.uint8
+FP8X4 = mybir.dt.float8_e4m3fn_x4
+FP4X4 = mybir.dt.float4_e2m1fn_x4
+COPY = mybir.ActivationFunctionType.Copy
+MULT = mybir.AluOpType.mult
+ADD = mybir.AluOpType.add
+MAX = mybir.AluOpType.max
+AXIS_X = mybir.AxisListType.X
+
+P = 128
+PACK = 4
+RUN = J // N
+QUARTER = U // 4
+BANK = 512
+Y_SPLIT = 320
+
+
+def weave_views(dst, src):
+    return (dst.rearrange("p (c i) t -> p c t i", i=4), src.rearrange("p t (c i) -> p c t i", i=4))
+
+
+def tile_attend_tab_lookedtimes_runsput_pl_kernel(tc, keys_words, keys_scales, notes, old, offs, offs2, offs3, offs4, out_0, out_1, out_2):
+    nc = tc.nc
+    with ExitStack() as ctx:
+        keep = ctx.enter_context(tc.tile_pool(name="keep", bufs=1))
+        psum = ctx.enter_context(tc.psum_pool(name="psum", bufs=1))
+
+        pool_words = keep.tile([P, T], U16, name="pool_words", align_bytes=64)
+        pool_scales = keep.tile([P, T], U8, name="pool_scales", align_bytes=64)
+        list1 = keep.tile([P, I // 16], U16, name="list1")
+        list2 = keep.tile([P, J // 16], U16, name="list2")
+        list3 = keep.tile([P, J // 16], U16, name="list3")
+        list4 = keep.tile([P, N // 16], U16, name="list4")
+
+        nc.gpsimd.memset(pool_scales[:].bitcast(I32), 0)
+        nc.sync.dma_start(pool_words[:].bitcast(I32), keys_words[0].bitcast(I32))
+        nc.sync.dma_start(list1[:], offs)
+        notes_rows = notes.rearrange("(p t) u -> p t u", t=PACK)
+        raw_quarters = []
+        for k in range(4):
+            raw = keep.tile([P, PACK, QUARTER], F32, name=f"notes_raw{k}", tag=f"staged{k}", align_bytes=64)
+            nc.sync.dma_start(raw[:], notes_rows[:, :, k * QUARTER : (k + 1) * QUARTER])
+            raw_quarters.append(raw[:])
+            if k == 0:
+                for q in range(4):
+                    nc.sync.dma_start(pool_scales[32 * q : 32 * q + 4, :].bitcast(I32), keys_scales[0, 4 * q : 4 * q + 4, :].bitcast(I32))
+        nc.sync.dma_start(list2[:], offs2)
+        nc.sync.dma_start(list3[:], offs3)
+        nc.sync.dma_start(list4[:], offs4)
+
+        placed = [keep.tile([P, M], F32, name=f"placed{t}", align_bytes=64) for t in range(PACK)]
+        for t in range(PACK):
+            nc.gpsimd.memset(placed[t][:], 0.0)
+
+        picked_words = keep.tile([P, I], U16, name="picked_words", align_bytes=64)
+        key_words = keep.tile([P, I], U16, name="key_words", align_bytes=64)
+        key_scales = keep.tile([P, I], U8, name="key_scales", align_bytes=64)
+        nc.vector.tensor_copy(picked_words[:], pool_words[:].indirect(list1[:]))
+        nc.vector.tensor_copy(key_words[:].rearrange("p (t s) -> p t s", t=PACK), picked_words[:].rearrange("p (s t) -> p t s", t=PACK))
+        nc.vector.tensor_copy(key_scales[:].rearrange("p (t s) -> p s t", t=PACK), pool_scales[:].indirect(list1[:]))
+
+        note_codes = [keep.tile([P, QUARTER], U32, name=f"note_codes{k}", align_bytes=64) for k in range(4)]
+        note_scales = [keep.tile([P, QUARTER], U8, name=f"note_scales{k}", align_bytes=64) for k in range(4)]
+        banks = [psum.tile([P, BANK], F32, name=f"bank{b}") for b in range(8)]
+        g1 = [keep.tile([P, U], F32, name=f"g1_{t}", align_bytes=64) for t in range(PACK)]
+        chunk_cols = (2 * QUARTER, QUARTER, QUARTER)
+        chunk_start = (0, 2 * QUARTER, 3 * QUARTER)
+
+        def sums(t, c):
+            if c == 0:
+                return banks[t][:]
+            return banks[2 + 2 * c + t // 2][:, (t % 2) * QUARTER : (t % 2 + 1) * QUARTER]
+
+        def multiply(k, tiles):
+            for t in tiles:
+                rows = slice(t * P, (t + 1) * P)
+                nc.tensor.matmul_mx(
+                    out=banks[t][:, k * QUARTER : (k + 1) * QUARTER] if k < 2 else sums(t, k - 1),
+                    lhsT=key_words[:, rows].bitcast(FP4X4),
+                    lhsT_scale=key_scales[:, rows],
+                    rhs=note_codes[k][:].bitcast(FP8X4),
+                    rhs_scale=note_scales[k][:],
+                    start=True,
+                    stop=True,
+                )
+
+        def table_part(t, c):
+            return g1[t][:, chunk_start[c] : chunk_start[c] + chunk_cols[c]]
+
+        woven = [keep.tile([P, QUARTER, PACK], BF16, name=f"woven{k}", align_bytes=64) for k in range(4)]
+
+        def weave_notes(k):
+            dst, src = weave_views(woven[k][:], raw_quarters[k])
+            if k == 0:
+                nc.scalar.activation(dst, src, COPY)
+            else:
+                nc.vector.tensor_copy(dst, src)
+
+        def quantise_notes(k):
+            nc.vector.quantize_mx(
+                out=note_codes[k][:].bitcast(FP8X4),
+                scales=note_scales[k][:],
+                in_=woven[k][:].rearrange("p c t -> p (c t)"),
+            )
+
+        weave_notes(0)
+        quantise_notes(0)
+        multiply(0, range(PACK))
+        weave_notes(1)
+        quantise_notes(1)
+        multiply(1, range(PACK))
+        weave_notes(2)
+        quantise_notes(2)
+        multiply(2, (0, 1))
+        weave_notes(3)
+        quantise_notes(3)
+        multiply(3, (0, 1))
+        multiply(2, (2, 3))
+        multiply(3, (2, 3))
+
+        old_rows = old.rearrange("(p t) m -> p t m", t=PACK)
+        old_sb = []
+        for k in range(2):
+            pair = keep.tile([P, 2, M], F32, name=f"old_pair{k}", tag=f"staged{k}", align_bytes=64)
+            nc.sync.dma_start(pair[:], old_rows[:, 2 * k : 2 * k + 2, :])
+            old_sb.extend([pair[:, 0, :], pair[:, 1, :]])
+
+        for t, c in ((0, 0), (0, 1), (1, 0), (1, 1), (2, 0), (3, 0)):
+            nc.scalar.copy(table_part(t, c), sums(t, c))
+        nc.vector.tensor_copy(table_part(0, 2), sums(0, 2))
+
+        left = [keep.tile([P, J], F32, name=f"left{t}", align_bytes=64) for t in range(PACK)]
+        g0 = [keep.tile([P, J], F32, name=f"g0_{t}", align_bytes=64) for t in range(PACK)]
+        best = [keep.tile([P, N], F32, name=f"best{t}", align_bytes=64) for t in range(PACK)]
+        y = keep.tile([P, PACK, M], F32, name="y", align_bytes=64)
+        out_rows = out_0.rearrange("(p t) m -> p t m", t=PACK)
+
+        right = [keep.tile([P, J], F32, name=f"right{k}", align_bytes=64) for k in range(2)]
+
+        def look_up_left(t):
+            if t > 1:
+                nc.scalar.copy(table_part(t, 1), sums(t, 1))
+            if t > 0:
+                nc.scalar.copy(table_part(t, 2), sums(t, 2))
+            nc.scalar.activation(left[t][:], g1[t][:].indirect(list2[:]), COPY)
+
+        def times_right(t):
+            if t == 0:
+                nc.vector.tensor_copy(right[0][:], g1[t][:].indirect(list3[:]))
+                nc.vector.tensor_tensor(g0[t][:], right[0][:], left[t][:], MULT)
+            elif t == PACK - 1:
+                nc.scalar.activation(right[1][:], g1[t][:].indirect(list3[:]), COPY)
+                nc.vector.tensor_tensor(g0[t][:], right[1][:], left[t][:], MULT)
+            else:
+                nc.vector.tensor_tensor(g0[t][:], g1[t][:].indirect(list3[:]), left[t][:], MULT)
+
+        def largest(t):
+            nc.vector.tensor_reduce(best[t][:], g0[t][:].rearrange("p (n r) -> p n r", r=RUN), AXIS_X, MAX)
+
+        def place(t):
+            if t == PACK - 1:
+                nc.vector.tensor_copy(placed[t][:].indirect(list4[:]), best[t][:])
+            else:
+                nc.scalar.activation(placed[t][:].indirect(list4[:]), best[t][:], COPY)
+
+        def add_old(t):
+            nc.vector.tensor_tensor(y[:, t, :], placed[t][:], old_sb[t], ADD)
+            nc.sync.dma_start(out_rows[:, t, :], y[:, t, :])
+
+        look_up_left(0)
+        look_up_left(1)
+        times_right(0)
+        largest(0)
+        look_up_left(2)
+        place(0)
+        times_right(1)
+        largest(1)
+        look_up_left(3)
+        place(1)
+        add_old(0)
+        times_right(2)
+        largest(2)
+        add_old(1)
+        times_right(3)
+        place(2)
+        largest(3)
+        add_old(2)
+        place(3)
+        add_old(3)
+
+        y_woven = keep.tile([P, M, PACK], BF16, name="y_woven", align_bytes=64)
+        y_codes = keep.tile([P, M], U32, name="y_codes", align_bytes=64)
+        y_scales = keep.tile([P, M], U8, name="y_scales", align_bytes=64)
+        dst, src = weave_views(y_woven[:, Y_SPLIT:M, :], y[:, :, Y_SPLIT:M])
+        nc.scalar.activation(dst, src, COPY)
+        dst, src = weave_views(y_woven[:, 0:Y_SPLIT, :], y[:, :, 0:Y_SPLIT])
+        nc.vector.tensor_copy(dst, src)
+        nc.vector.quantize_mx(out=y_codes[:].bitcast(FP8X4), scales=y_scales[:], in_=y_woven[:].rearrange("p c t -> p (c t)"))
+        nc.sync.dma_start(out_1[0].rearrange("p c t -> p (c t)").bitcast(I32), y_codes[:].bitcast(I32))
+        for q in range(4):
+            queue = nc.scalar if q % 2 == 0 else nc.sync
+            queue.dma_start(out_2[0, 4 * q : 4 * q + 4, :].bitcast(I32), y_scales[32 * q : 32 * q + 4, :].bitcast(I32))

@@ -24,7 +24,7 @@ PACK = 4
 RUN = J // N
 QUARTER = U // 4
 BANK = 512
-Y_SPLIT = 320
+HALF = M // 2
 
 
 def weave_views(dst, src):
@@ -75,19 +75,15 @@ def tile_attend_tab_lookedtimes_runsput_pl_kernel(tc, keys_words, keys_scales, n
         note_scales = [keep.tile([P, QUARTER], U8, name=f"note_scales{k}", align_bytes=64) for k in range(4)]
         banks = [psum.tile([P, BANK], F32, name=f"bank{b}") for b in range(8)]
         g1 = [keep.tile([P, U], F32, name=f"g1_{t}", align_bytes=64) for t in range(PACK)]
-        chunk_cols = (2 * QUARTER, QUARTER, QUARTER)
-        chunk_start = (0, 2 * QUARTER, 3 * QUARTER)
 
-        def sums(t, c):
-            if c == 0:
-                return banks[t][:]
-            return banks[2 + 2 * c + t // 2][:, (t % 2) * QUARTER : (t % 2 + 1) * QUARTER]
+        def sums(t, k):
+            return banks[2 * k + t // 2][:, (t % 2) * QUARTER : (t % 2 + 1) * QUARTER]
 
         def multiply(k, tiles):
             for t in tiles:
                 rows = slice(t * P, (t + 1) * P)
                 nc.tensor.matmul_mx(
-                    out=banks[t][:, k * QUARTER : (k + 1) * QUARTER] if k < 2 else sums(t, k - 1),
+                    out=sums(t, k),
                     lhsT=key_words[:, rows].bitcast(FP4X4),
                     lhsT_scale=key_scales[:, rows],
                     rhs=note_codes[k][:].bitcast(FP8X4),
@@ -96,14 +92,14 @@ def tile_attend_tab_lookedtimes_runsput_pl_kernel(tc, keys_words, keys_scales, n
                     stop=True,
                 )
 
-        def table_part(t, c):
-            return g1[t][:, chunk_start[c] : chunk_start[c] + chunk_cols[c]]
+        def table_part(t, k):
+            return g1[t][:, k * QUARTER : (k + 1) * QUARTER]
 
         woven = [keep.tile([P, QUARTER, PACK], BF16, name=f"woven{k}", align_bytes=64) for k in range(4)]
 
         def weave_notes(k):
             dst, src = weave_views(woven[k][:], raw_quarters[k])
-            if k == 0:
+            if k < 2:
                 nc.scalar.activation(dst, src, COPY)
             else:
                 nc.vector.tensor_copy(dst, src)
@@ -137,32 +133,31 @@ def tile_attend_tab_lookedtimes_runsput_pl_kernel(tc, keys_words, keys_scales, n
             nc.sync.dma_start(pair[:], old_rows[:, 2 * k : 2 * k + 2, :])
             old_sb.extend([pair[:, 0, :], pair[:, 1, :]])
 
-        for t, c in ((0, 0), (0, 1), (1, 0), (1, 1), (2, 0), (3, 0)):
-            nc.scalar.copy(table_part(t, c), sums(t, c))
-        nc.vector.tensor_copy(table_part(0, 2), sums(0, 2))
-
         left = [keep.tile([P, J], F32, name=f"left{t}", align_bytes=64) for t in range(PACK)]
         g0 = [keep.tile([P, J], F32, name=f"g0_{t}", align_bytes=64) for t in range(PACK)]
         best = [keep.tile([P, N], F32, name=f"best{t}", align_bytes=64) for t in range(PACK)]
         y = keep.tile([P, PACK, M], F32, name="y", align_bytes=64)
         out_rows = out_0.rearrange("(p t) m -> p t m", t=PACK)
 
-        right = [keep.tile([P, J], F32, name=f"right{k}", align_bytes=64) for k in range(2)]
+        right_last = keep.tile([P, J], F32, name="right_last", align_bytes=64)
+
+        def fill_table(t):
+            for k in range(4):
+                if t == 0 and k >= 2:
+                    nc.vector.tensor_copy(table_part(t, k), sums(t, k))
+                else:
+                    nc.scalar.copy(table_part(t, k), sums(t, k))
 
         def look_up_left(t):
-            if t > 1:
-                nc.scalar.copy(table_part(t, 1), sums(t, 1))
-            if t > 0:
-                nc.scalar.copy(table_part(t, 2), sums(t, 2))
-            nc.scalar.activation(left[t][:], g1[t][:].indirect(list2[:]), COPY)
+            if t == 0:
+                nc.vector.tensor_copy(left[t][:], g1[t][:].indirect(list2[:]))
+            else:
+                nc.scalar.activation(left[t][:], g1[t][:].indirect(list2[:]), COPY)
 
         def times_right(t):
-            if t == 0:
-                nc.vector.tensor_copy(right[0][:], g1[t][:].indirect(list3[:]))
-                nc.vector.tensor_tensor(g0[t][:], right[0][:], left[t][:], MULT)
-            elif t == PACK - 1:
-                nc.scalar.activation(right[1][:], g1[t][:].indirect(list3[:]), COPY)
-                nc.vector.tensor_tensor(g0[t][:], right[1][:], left[t][:], MULT)
+            if t == PACK - 1:
+                nc.scalar.activation(right_last[:], g1[t][:].indirect(list3[:]), COPY)
+                nc.vector.tensor_tensor(g0[t][:], right_last[:], left[t][:], MULT)
             else:
                 nc.vector.tensor_tensor(g0[t][:], g1[t][:].indirect(list3[:]), left[t][:], MULT)
 
@@ -170,45 +165,56 @@ def tile_attend_tab_lookedtimes_runsput_pl_kernel(tc, keys_words, keys_scales, n
             nc.vector.tensor_reduce(best[t][:], g0[t][:].rearrange("p (n r) -> p n r", r=RUN), AXIS_X, MAX)
 
         def place(t):
-            if t == PACK - 1:
-                nc.vector.tensor_copy(placed[t][:].indirect(list4[:]), best[t][:])
-            else:
-                nc.scalar.activation(placed[t][:].indirect(list4[:]), best[t][:], COPY)
+            nc.scalar.activation(placed[t][:].indirect(list4[:]), best[t][:], COPY)
 
-        def add_old(t):
-            nc.vector.tensor_tensor(y[:, t, :], placed[t][:], old_sb[t], ADD)
+        def add_old(t, cols):
+            nc.vector.tensor_tensor(y[:, t, cols], placed[t][:, cols], old_sb[t][:, cols], ADD)
+
+        def store_rows(t):
             nc.sync.dma_start(out_rows[:, t, :], y[:, t, :])
 
+        whole, low, high = slice(0, M), slice(0, HALF), slice(HALF, M)
+        fill_table(0)
         look_up_left(0)
+        fill_table(1)
         look_up_left(1)
         times_right(0)
         largest(0)
+        fill_table(2)
         look_up_left(2)
-        place(0)
         times_right(1)
         largest(1)
+        fill_table(3)
         look_up_left(3)
-        place(1)
-        add_old(0)
+        place(0)
         times_right(2)
         largest(2)
-        add_old(1)
         times_right(3)
+        place(1)
         place(2)
+        add_old(0, whole)
+        store_rows(0)
         largest(3)
-        add_old(2)
+        add_old(1, whole)
+        store_rows(1)
         place(3)
-        add_old(3)
+        add_old(2, whole)
+        store_rows(2)
+        add_old(3, high)
+        add_old(3, low)
+        store_rows(3)
 
         y_woven = keep.tile([P, M, PACK], BF16, name="y_woven", align_bytes=64)
         y_codes = keep.tile([P, M], U32, name="y_codes", align_bytes=64)
         y_scales = keep.tile([P, M], U8, name="y_scales", align_bytes=64)
-        dst, src = weave_views(y_woven[:, Y_SPLIT:M, :], y[:, :, Y_SPLIT:M])
+        dst, src = weave_views(y_woven[:, high, :], y[:, :, high])
         nc.scalar.activation(dst, src, COPY)
-        dst, src = weave_views(y_woven[:, 0:Y_SPLIT, :], y[:, :, 0:Y_SPLIT])
+        dst, src = weave_views(y_woven[:, low, :], y[:, :, low])
         nc.vector.tensor_copy(dst, src)
-        nc.vector.quantize_mx(out=y_codes[:].bitcast(FP8X4), scales=y_scales[:], in_=y_woven[:].rearrange("p c t -> p (c t)"))
-        nc.sync.dma_start(out_1[0].rearrange("p c t -> p (c t)").bitcast(I32), y_codes[:].bitcast(I32))
+        code_rows = out_1[0].rearrange("p c t -> p (c t)").bitcast(I32)
+        for cols in (low, high):
+            nc.vector.quantize_mx(out=y_codes[:, cols].bitcast(FP8X4), scales=y_scales[:, cols], in_=y_woven[:, cols, :].rearrange("p c t -> p (c t)"))
+            nc.sync.dma_start(code_rows[:, cols], y_codes[:, cols].bitcast(I32))
         for q in range(4):
-            queue = nc.scalar if q % 2 == 0 else nc.sync
+            queue = nc.scalar if q < 3 else nc.sync
             queue.dma_start(out_2[0, 4 * q : 4 * q + 4, :].bitcast(I32), y_scales[32 * q : 32 * q + 4, :].bitcast(I32))

@@ -71,29 +71,33 @@ def tile_attend_tab_lookedtimes_runsput_pl_kernel(tc, keys_words, keys_scales, n
         nc.vector.tensor_copy(key_words[:].rearrange("p (t s) -> p t s", t=PACK), picked_words[:].rearrange("p (s t) -> p t s", t=PACK))
         nc.vector.tensor_copy(key_scales[:].rearrange("p (t s) -> p s t", t=PACK), pool_scales[:].indirect(list1[:]))
 
-        note_codes = [keep.tile([P, QUARTER], U32, name=f"note_codes{k}", align_bytes=64) for k in range(4)]
-        note_scales = [keep.tile([P, QUARTER], U8, name=f"note_scales{k}", align_bytes=64) for k in range(4)]
-        banks = [psum.tile([P, BANK], F32, name=f"bank{b}") for b in range(8)]
+        note_codes = [keep.tile([P, BANK], U32, name=f"note_codes{h}", align_bytes=64) for h in range(2)]
+        note_scales = [keep.tile([P, BANK], U8, name=f"note_scales{h}", align_bytes=64) for h in range(2)]
         g1 = [keep.tile([P, U], F32, name=f"g1_{t}", align_bytes=64) for t in range(PACK)]
 
-        def sums(t, k):
-            return banks[2 * k + t // 2][:, (t % 2) * QUARTER : (t % 2 + 1) * QUARTER]
+        def multiply(sums, t, h, cols):
+            rows = slice(t * P, (t + 1) * P)
+            nc.tensor.matmul_mx(
+                out=sums,
+                lhsT=key_words[:, rows].bitcast(FP4X4),
+                lhsT_scale=key_scales[:, rows],
+                rhs=note_codes[h][:, cols].bitcast(FP8X4),
+                rhs_scale=note_scales[h][:, cols],
+                start=True,
+                stop=True,
+            )
 
-        def multiply(k, tiles):
-            for t in tiles:
-                rows = slice(t * P, (t + 1) * P)
-                nc.tensor.matmul_mx(
-                    out=sums(t, k),
-                    lhsT=key_words[:, rows].bitcast(FP4X4),
-                    lhsT_scale=key_scales[:, rows],
-                    rhs=note_codes[k][:].bitcast(FP8X4),
-                    rhs_scale=note_scales[k][:],
-                    start=True,
-                    stop=True,
-                )
+        def cols_in_half(k):
+            return slice((k % 2) * QUARTER, (k % 2 + 1) * QUARTER)
 
-        def table_part(t, k):
-            return g1[t][:, k * QUARTER : (k + 1) * QUARTER]
+        pair_banks = {}
+        for k in range(4):
+            for pair in range(2 if k < 2 else 1):
+                pair_banks[pair, k] = psum.tile([P, 2, QUARTER], F32, name=f"pair{pair}_{k}")
+        half_banks = {t: psum.tile([P, BANK], F32, name=f"half{t}") for t in (2, 3)}
+
+        def quarter_sums(t, k):
+            return pair_banks[t // 2, k][:, t % 2, :]
 
         woven = [keep.tile([P, QUARTER, PACK], BF16, name=f"woven{k}", align_bytes=64) for k in range(4)]
 
@@ -106,25 +110,18 @@ def tile_attend_tab_lookedtimes_runsput_pl_kernel(tc, keys_words, keys_scales, n
 
         def quantise_notes(k):
             nc.vector.quantize_mx(
-                out=note_codes[k][:].bitcast(FP8X4),
-                scales=note_scales[k][:],
+                out=note_codes[k // 2][:, cols_in_half(k)].bitcast(FP8X4),
+                scales=note_scales[k // 2][:, cols_in_half(k)],
                 in_=woven[k][:].rearrange("p c t -> p (c t)"),
             )
 
-        weave_notes(0)
-        quantise_notes(0)
-        multiply(0, range(PACK))
-        weave_notes(1)
-        quantise_notes(1)
-        multiply(1, range(PACK))
-        weave_notes(2)
-        quantise_notes(2)
-        multiply(2, (0, 1))
-        weave_notes(3)
-        quantise_notes(3)
-        multiply(3, (0, 1))
-        multiply(2, (2, 3))
-        multiply(3, (2, 3))
+        for k in range(4):
+            weave_notes(k)
+            quantise_notes(k)
+            for t in range(4 if k < 2 else 2):
+                multiply(quarter_sums(t, k), t, k // 2, cols_in_half(k))
+        for t in (2, 3):
+            multiply(half_banks[t][:], t, 1, slice(0, BANK))
 
         old_rows = old.rearrange("(p t) m -> p t m", t=PACK)
         old_sb = []
@@ -139,14 +136,17 @@ def tile_attend_tab_lookedtimes_runsput_pl_kernel(tc, keys_words, keys_scales, n
         y = keep.tile([P, PACK, M], F32, name="y", align_bytes=64)
         out_rows = out_0.rearrange("(p t) m -> p t m", t=PACK)
 
-        right_last = keep.tile([P, J], F32, name="right_last", align_bytes=64)
+        right = {t: keep.tile([P, J], F32, name=f"right{t}", align_bytes=64) for t in (2, 3)}
 
         def fill_table(t):
-            for k in range(4):
-                if t == 0 and k >= 2:
-                    nc.vector.tensor_copy(table_part(t, k), sums(t, k))
+            for k in range(4 if t < 2 else 2):
+                part = g1[t][:, k * QUARTER : (k + 1) * QUARTER]
+                if k == 3:
+                    nc.vector.tensor_copy(part, quarter_sums(t, k))
                 else:
-                    nc.scalar.copy(table_part(t, k), sums(t, k))
+                    nc.scalar.copy(part, quarter_sums(t, k))
+            if t >= 2:
+                nc.scalar.copy(g1[t][:, BANK:U], half_banks[t][:])
 
         def look_up_left(t):
             if t == 0:
@@ -154,10 +154,12 @@ def tile_attend_tab_lookedtimes_runsput_pl_kernel(tc, keys_words, keys_scales, n
             else:
                 nc.scalar.activation(left[t][:], g1[t][:].indirect(list2[:]), COPY)
 
+        def look_up_right(t):
+            nc.scalar.activation(right[t][:], g1[t][:].indirect(list3[:]), COPY)
+
         def times_right(t):
-            if t == PACK - 1:
-                nc.scalar.activation(right_last[:], g1[t][:].indirect(list3[:]), COPY)
-                nc.vector.tensor_tensor(g0[t][:], right_last[:], left[t][:], MULT)
+            if t in right:
+                nc.vector.tensor_tensor(g0[t][:], right[t][:], left[t][:], MULT)
             else:
                 nc.vector.tensor_tensor(g0[t][:], g1[t][:].indirect(list3[:]), left[t][:], MULT)
 
@@ -165,7 +167,10 @@ def tile_attend_tab_lookedtimes_runsput_pl_kernel(tc, keys_words, keys_scales, n
             nc.vector.tensor_reduce(best[t][:], g0[t][:].rearrange("p (n r) -> p n r", r=RUN), AXIS_X, MAX)
 
         def place(t):
-            nc.scalar.activation(placed[t][:].indirect(list4[:]), best[t][:], COPY)
+            if t == 0:
+                nc.vector.tensor_copy(placed[t][:].indirect(list4[:]), best[t][:])
+            else:
+                nc.scalar.activation(placed[t][:].indirect(list4[:]), best[t][:], COPY)
 
         def add_old(t, cols):
             nc.vector.tensor_tensor(y[:, t, cols], placed[t][:, cols], old_sb[t][:, cols], ADD)
@@ -182,22 +187,24 @@ def tile_attend_tab_lookedtimes_runsput_pl_kernel(tc, keys_words, keys_scales, n
         largest(0)
         fill_table(2)
         look_up_left(2)
+        look_up_right(2)
         times_right(1)
         largest(1)
         fill_table(3)
         look_up_left(3)
+        look_up_right(3)
         place(0)
         times_right(2)
         largest(2)
+        add_old(0, whole)
+        store_rows(0)
         times_right(3)
         place(1)
         place(2)
-        add_old(0, whole)
-        store_rows(0)
         largest(3)
+        place(3)
         add_old(1, whole)
         store_rows(1)
-        place(3)
         add_old(2, whole)
         store_rows(2)
         add_old(3, high)

from contextlib import ExitStack

import concourse.mybir as mybir

D, T, I, J, U, M, N = 512, 2048, 512, 512, 1024, 512, 64
FLOPS = 2 * D * I * U

F32 = mybir.dt.float32
BF16 = mybir.dt.bfloat16
I32 = mybir.dt.int32
U32 = mybir.dt.uint32
U16 = mybir.dt.uint16
U8 = mybir.dt.uint8
FP8X4 = mybir.dt.float8_e4m3fn_x4
FP4X4 = mybir.dt.float4_e2m1fn_x4
COPY = mybir.ActivationFunctionType.Copy
MULT = mybir.AluOpType.mult
ADD = mybir.AluOpType.add
MAX = mybir.AluOpType.max
AXIS_X = mybir.AxisListType.X

P = 128
PACK = 4
RUN = J // N
QUARTER = U // 4
BANK = 512
HALF = M // 2


def weave_views(dst, src):
    return (dst.rearrange("p (c i) t -> p c t i", i=4), src.rearrange("p t (c i) -> p c t i", i=4))


def tile_attend_tab_lookedtimes_runsput_pl_kernel(tc, keys_words, keys_scales, notes, old, offs, offs2, offs3, offs4, out_0, out_1, out_2):
    nc = tc.nc
    with ExitStack() as ctx:
        keep = ctx.enter_context(tc.tile_pool(name="keep", bufs=1))
        psum = ctx.enter_context(tc.psum_pool(name="psum", bufs=1))

        pool_words = keep.tile([P, T], U16, name="pool_words", align_bytes=64)
        pool_scales = keep.tile([P, T], U8, name="pool_scales", align_bytes=64)
        list1 = keep.tile([P, I // 16], U16, name="list1")
        list2 = keep.tile([P, J // 16], U16, name="list2")
        list3 = keep.tile([P, J // 16], U16, name="list3")
        list4 = keep.tile([P, N // 16], U16, name="list4")

        nc.gpsimd.memset(pool_scales[:].bitcast(I32), 0)
        nc.sync.dma_start(pool_words[:].bitcast(I32), keys_words[0].bitcast(I32))
        nc.sync.dma_start(list1[:], offs)
        notes_rows = notes.rearrange("(p t) u -> p t u", t=PACK)
        raw_quarters = []
        for k in range(4):
            raw = keep.tile([P, PACK, QUARTER], F32, name=f"notes_raw{k}", tag=f"staged{k}", align_bytes=64)
            nc.sync.dma_start(raw[:], notes_rows[:, :, k * QUARTER : (k + 1) * QUARTER])
            raw_quarters.append(raw[:])
            if k == 0:
                for q in range(4):
                    nc.sync.dma_start(pool_scales[32 * q : 32 * q + 4, :].bitcast(I32), keys_scales[0, 4 * q : 4 * q + 4, :].bitcast(I32))
        nc.sync.dma_start(list2[:], offs2)
        nc.sync.dma_start(list3[:], offs3)
        nc.sync.dma_start(list4[:], offs4)

        placed = [keep.tile([P, M], F32, name=f"placed{t}", align_bytes=64) for t in range(PACK)]
        for t in range(PACK):
            nc.gpsimd.memset(placed[t][:], 0.0)

        picked_words = keep.tile([P, I], U16, name="picked_words", align_bytes=64)
        key_words = keep.tile([P, I], U16, name="key_words", align_bytes=64)
        key_scales = keep.tile([P, I], U8, name="key_scales", align_bytes=64)
        nc.vector.tensor_copy(picked_words[:], pool_words[:].indirect(list1[:]))
        nc.vector.tensor_copy(key_words[:].rearrange("p (t s) -> p t s", t=PACK), picked_words[:].rearrange("p (s t) -> p t s", t=PACK))
        nc.vector.tensor_copy(key_scales[:].rearrange("p (t s) -> p s t", t=PACK), pool_scales[:].indirect(list1[:]))

        note_codes = [keep.tile([P, BANK], U32, name=f"note_codes{h}", align_bytes=64) for h in range(2)]
        note_scales = [keep.tile([P, BANK], U8, name=f"note_scales{h}", align_bytes=64) for h in range(2)]
        g1 = [keep.tile([P, U], F32, name=f"g1_{t}", align_bytes=64) for t in range(PACK)]

        def multiply(sums, t, h, cols):
            rows = slice(t * P, (t + 1) * P)
            nc.tensor.matmul_mx(
                out=sums,
                lhsT=key_words[:, rows].bitcast(FP4X4),
                lhsT_scale=key_scales[:, rows],
                rhs=note_codes[h][:, cols].bitcast(FP8X4),
                rhs_scale=note_scales[h][:, cols],
                start=True,
                stop=True,
            )

        def cols_in_half(k):
            return slice((k % 2) * QUARTER, (k % 2 + 1) * QUARTER)

        pair_banks = {}
        for k in range(4):
            for pair in range(2 if k < 2 else 1):
                pair_banks[pair, k] = psum.tile([P, 2, QUARTER], F32, name=f"pair{pair}_{k}")
        half_banks = {t: psum.tile([P, BANK], F32, name=f"half{t}") for t in (2, 3)}

        def quarter_sums(t, k):
            return pair_banks[t // 2, k][:, t % 2, :]

        woven = [keep.tile([P, QUARTER, PACK], BF16, name=f"woven{k}", align_bytes=64) for k in range(4)]

        def weave_notes(k):
            dst, src = weave_views(woven[k][:], raw_quarters[k])
            if k < 2:
                nc.scalar.activation(dst, src, COPY)
            else:
                nc.vector.tensor_copy(dst, src)

        def quantise_notes(k):
            nc.vector.quantize_mx(
                out=note_codes[k // 2][:, cols_in_half(k)].bitcast(FP8X4),
                scales=note_scales[k // 2][:, cols_in_half(k)],
                in_=woven[k][:].rearrange("p c t -> p (c t)"),
            )

        for k in range(4):
            weave_notes(k)
            quantise_notes(k)
            for t in range(4 if k < 2 else 2):
                multiply(quarter_sums(t, k), t, k // 2, cols_in_half(k))
        for t in (2, 3):
            multiply(half_banks[t][:], t, 1, slice(0, BANK))

        old_rows = old.rearrange("(p t) m -> p t m", t=PACK)
        old_sb = []
        for k in range(2):
            pair = keep.tile([P, 2, M], F32, name=f"old_pair{k}", tag=f"staged{k}", align_bytes=64)
            nc.sync.dma_start(pair[:], old_rows[:, 2 * k : 2 * k + 2, :])
            old_sb.extend([pair[:, 0, :], pair[:, 1, :]])

        left = [keep.tile([P, J], F32, name=f"left{t}", align_bytes=64) for t in range(PACK)]
        g0 = [keep.tile([P, J], F32, name=f"g0_{t}", align_bytes=64) for t in range(PACK)]
        best = [keep.tile([P, N], F32, name=f"best{t}", align_bytes=64) for t in range(PACK)]
        y = keep.tile([P, PACK, M], F32, name="y", align_bytes=64)
        out_rows = out_0.rearrange("(p t) m -> p t m", t=PACK)

        right = {t: keep.tile([P, J], F32, name=f"right{t}", align_bytes=64) for t in (2, 3)}

        def fill_table(t):
            for k in range(4 if t < 2 else 2):
                part = g1[t][:, k * QUARTER : (k + 1) * QUARTER]
                if k == 3:
                    nc.vector.tensor_copy(part, quarter_sums(t, k))
                else:
                    nc.scalar.copy(part, quarter_sums(t, k))
            if t >= 2:
                nc.scalar.copy(g1[t][:, BANK:U], half_banks[t][:])

        def look_up_left(t):
            if t == 0:
                nc.vector.tensor_copy(left[t][:], g1[t][:].indirect(list2[:]))
            else:
                nc.scalar.activation(left[t][:], g1[t][:].indirect(list2[:]), COPY)

        def look_up_right(t):
            nc.scalar.activation(right[t][:], g1[t][:].indirect(list3[:]), COPY)

        def times_right(t):
            if t in right:
                nc.vector.tensor_tensor(g0[t][:], right[t][:], left[t][:], MULT)
            else:
                nc.vector.tensor_tensor(g0[t][:], g1[t][:].indirect(list3[:]), left[t][:], MULT)

        def largest(t):
            nc.vector.tensor_reduce(best[t][:], g0[t][:].rearrange("p (n r) -> p n r", r=RUN), AXIS_X, MAX)

        def place(t):
            if t == 0:
                nc.vector.tensor_copy(placed[t][:].indirect(list4[:]), best[t][:])
            else:
                nc.scalar.activation(placed[t][:].indirect(list4[:]), best[t][:], COPY)

        def add_old(t, cols):
            nc.vector.tensor_tensor(y[:, t, cols], placed[t][:, cols], old_sb[t][:, cols], ADD)

        def store_rows(t):
            nc.sync.dma_start(out_rows[:, t, :], y[:, t, :])

        whole, low, high = slice(0, M), slice(0, HALF), slice(HALF, M)
        fill_table(0)
        look_up_left(0)
        fill_table(1)
        look_up_left(1)
        times_right(0)
        largest(0)
        fill_table(2)
        look_up_left(2)
        look_up_right(2)
        times_right(1)
        largest(1)
        fill_table(3)
        look_up_left(3)
        look_up_right(3)
        place(0)
        times_right(2)
        largest(2)
        add_old(0, whole)
        store_rows(0)
        times_right(3)
        place(1)
        place(2)
        largest(3)
        place(3)
        add_old(1, whole)
        store_rows(1)
        add_old(2, whole)
        store_rows(2)
        add_old(3, high)
        add_old(3, low)
        store_rows(3)

        y_woven = keep.tile([P, M, PACK], BF16, name="y_woven", align_bytes=64)
        y_codes = keep.tile([P, M], U32, name="y_codes", align_bytes=64)
        y_scales = keep.tile([P, M], U8, name="y_scales", align_bytes=64)
        dst, src = weave_views(y_woven[:, high, :], y[:, :, high])
        nc.scalar.activation(dst, src, COPY)
        dst, src = weave_views(y_woven[:, low, :], y[:, :, low])
        nc.vector.tensor_copy(dst, src)
        code_rows = out_1[0].rearrange("p c t -> p (c t)").bitcast(I32)
        for cols in (low, high):
            nc.vector.quantize_mx(out=y_codes[:, cols].bitcast(FP8X4), scales=y_scales[:, cols], in_=y_woven[:, cols, :].rearrange("p c t -> p (c t)"))
            nc.sync.dma_start(code_rows[:, cols], y_codes[:, cols].bitcast(I32))
        for q in range(4):
            queue = nc.scalar if q < 3 else nc.sync
            queue.dma_start(out_2[0, 4 * q : 4 * q + 4, :].bitcast(I32), y_scales[32 * q : 32 * q + 4, :].bitcast(I32))
